import numpy as np
import ml_dtypes


def mxq(x, axis, fmt="e4m3"):
    dtype, down = {"e4m3": (ml_dtypes.float8_e4m3fn, 7), "e5m2": (ml_dtypes.float8_e5m2, 14)}[fmt]
    v = np.moveaxis(np.asarray(x, np.float32).astype(ml_dtypes.bfloat16).astype(np.float64), axis, -1)
    blocks = v.reshape(v.shape[:-1] + (-1, 32))
    amax = np.abs(blocks).max(-1, keepdims=True)
    byte = np.maximum(np.where(amax > 0, np.frexp(amax)[1] - 1 + 127, 0) - down, 1)
    scale = np.exp2(byte - 127.0)
    codes = (blocks / scale).astype(np.float32).astype(dtype).astype(np.float64)
    return np.moveaxis((codes * scale).reshape(v.shape), -1, axis)


WIDE = False


def mx_kscale(k):
    if not WIDE:
        return np.ones(k)
    levels = np.array([10, -10, 5, -5, 0])
    if k % 512:
        return np.exp2(np.random.permutation(np.resize(levels, k // 32))).repeat(32)
    a = np.empty((k // 512, 16))
    for p in range(k // 512):
        a[p, :8] = np.random.permutation(np.resize(levels, 8))
        for g in range(8):
            far = levels[np.abs(levels - a[p, g]) >= 10]
            a[p, g + 8] = far[np.random.randint(len(far))]
    return np.exp2(a.ravel()).repeat(32)


def f64(x):
    return np.asarray(x).astype(np.float64)


E2M1 = np.array([0.0, 0.5, 1.0, 1.5, 2.0, 3.0, 4.0, 6.0, -0.0, -0.5, -1.0, -1.5, -2.0, -3.0, -4.0, -6.0])


def pack_weight(w, fmt):
    k, n = w.shape
    w = f64(np.asarray(w, np.float32).astype(ml_dtypes.bfloat16)).reshape(k // 32, 32, n)
    amax = np.abs(w).max(1)
    if fmt == "e4m3":
        byte = np.frexp(amax)[1] - 1 + 127 - 7
    else:
        mant, ex = np.frexp(amax / 6.0)
        byte = np.where(mant > 0.5, ex, ex - 1) + 127
    byte = np.clip(np.where(amax > 0, byte, 1), 1, 254)
    scaled = (w * np.exp2(127.0 - byte)[:, None, :]).reshape(k, n).astype(np.float32)
    by_word = np.ascontiguousarray(scaled.reshape(k // 512, 128, 4, n).transpose(0, 1, 3, 2))
    if fmt == "e4m3":
        words = by_word.astype(ml_dtypes.float8_e4m3fn).view(np.uint8)
    else:
        c = by_word.astype(ml_dtypes.float4_e2m1fn).view(np.uint8) & 0xF
        words = (c[..., 0::2] | (c[..., 1::2] << 4)).reshape(k // 512, 128, 2 * n)
    return np.ascontiguousarray(words), np.ascontiguousarray(byte.astype(np.uint8).reshape(k // 512, 16, n))


def unpack_weight(words, scales, fmt):
    g, _, n = scales.shape
    words = np.ascontiguousarray(words).reshape(g, 128, n, -1)
    if fmt == "e4m3":
        vals = words.view(ml_dtypes.float8_e4m3fn).astype(np.float64)
    else:
        nib = np.empty((g, 128, n, 4), np.uint8)
        nib[..., 0::2] = words & 0xF
        nib[..., 1::2] = words >> 4
        vals = E2M1[nib]
    vals = vals * np.repeat(np.exp2(scales.astype(np.float64) - 127.0), 8, axis=1)[..., None]
    return vals.transpose(0, 1, 3, 2).reshape(g * 512, n)


O, K, M, T = 512, 2048, 512, 1536


def setup_inputs():
    n = np.random.standard_normal
    s = mx_kscale(K)[:, None]
    x = n((K, T)); x[:O] *= 6.0
    w = n((K, M)) / np.sqrt(K) / s; w[:O] /= 2.0
    p_w8 = pack_weight(w[:O], "e4m3")
    p_w4 = pack_weight(w[O:], "e2m1")
    return {
        "x": (x * s).astype(np.float32),
        "w8_words": p_w8[0],
        "w8_scales": p_w8[1],
        "w4_words": p_w4[0],
        "w4_scales": p_w4[1],
        "r": (n((1536, 512))).astype(np.float32),
    }


def reference(x, w8_words, w8_scales, w4_words, w4_scales, r):
    x_ = mxq(f64(x), 0, "e4m3")
    w8_ = unpack_weight(w8_words, w8_scales, "e4m3")
    w4_ = unpack_weight(w4_words, w4_scales, "e2m1")
    y = x_[:O].T @ w8_ + x_[O:].T @ w4_
    return f64(r) + y

@@ -1,0 +1,152 @@
+from contextlib import ExitStack
+
+import concourse.mybir as mybir
+
+F32 = mybir.dt.float32
+BF16 = mybir.dt.bfloat16
+I32 = mybir.dt.int32
+U32 = mybir.dt.uint32
+U8 = mybir.dt.uint8
+FP8X4 = mybir.dt.float8_e4m3fn_x4
+FP4X4 = mybir.dt.float4_e2m1fn_x4
+
+P = 128
+K, T, N = 2048, 1536, 512
+PACK = 4
+K_PASS = P * PACK
+PASSES = K // K_PASS
+UNIT = 512
+SLOTS = UNIT // P
+UNITS = T // UNIT
+BANKS = 8
+VECTOR_M = 80
+
+FLOPS = 2 * K * T * N
+
+
+def tile_mix_outl_tm_res_kernel(tc, x, w8_words, w8_scales, w4_words, w4_scales, r, out):
+    nc = tc.nc
+    with ExitStack() as ctx:
+        keep = ctx.enter_context(tc.tile_pool(name="keep", bufs=1))
+        psum = ctx.enter_context(tc.psum_pool(name="psum", bufs=1))
+        ctx.enter_context(tc.manual_schedule())
+
+        def load_x(g, first, count):
+            width = count * UNIT
+            t = keep.tile([P, PACK, width], F32, name="x%d_%d" % (g, first))
+            rows = x[g * K_PASS : (g + 1) * K_PASS, :].rearrange("(p i) t -> p i t", i=PACK)
+            nc.sync.dma_start(out=t[:], in_=rows[:, :, first * UNIT : first * UNIT + width])
+            for u in range(first, first + count):
+                raw[g, u] = t[:, :, (u - first) * UNIT : (u - first + 1) * UNIT]
+
+        def load_r(u, first, count):
+            rows = r[u * UNIT : (u + 1) * UNIT, :].rearrange("(m q) n -> m q n", q=SLOTS)
+            nc.sync.dma_start(out=r_sb[u][:, first : first + count, :], in_=rows[:, first : first + count, :])
+
+        def store(u, first, count):
+            rows = out[u * UNIT : (u + 1) * UNIT, :].rearrange("(m q) n -> m q n", q=SLOTS)
+            nc.sync.dma_start(out=rows[:, first : first + count, :], in_=o_sb[u][:, first : first + count, :])
+
+        raw = {}
+        grouped = {}
+        codes = {}
+        scales = {}
+        r_sb = {}
+        o_sb = {}
+        acc = {}
+        for u in range(UNITS):
+            r_sb[u] = keep.tile([P, SLOTS, N], F32, name="r%d" % u)
+            o_sb[u] = keep.tile([P, SLOTS, N], F32, name="o%d" % u)
+        w8 = keep.tile([P, 4 * N], U8, name="w8", align_bytes=64)
+        w4 = keep.tile([P, PASSES - 1, 2 * N], U8, name="w4", align_bytes=64)
+        w_scale = keep.tile([P, PASSES, N], U8, name="w_scale", align_bytes=64)
+
+        def copy(g, u):
+            t = keep.tile([P, UNIT * PACK], BF16, name="b%d_%d" % (g, u), align_bytes=64)
+            dst = t[:].rearrange("p (q m i) -> p m i q", q=SLOTS, i=PACK)
+            src = raw[g, u].rearrange("p i (m q) -> p m i q", q=SLOTS)
+            nc.vector.tensor_copy(out=dst[:, :VECTOR_M], in_=src[:, :VECTOR_M])
+            nc.scalar.copy(out=dst[:, VECTOR_M:], in_=src[:, VECTOR_M:])
+            grouped[g, u] = t
+
+        def quantise(g, u):
+            c = keep.tile([P, UNIT], U32, name="c%d_%d" % (g, u), align_bytes=64)
+            s = keep.tile([P, UNIT], U8, name="s%d_%d" % (g, u), align_bytes=64)
+            nc.vector.quantize_mx(out=c[:].bitcast(FP8X4), scales=s[:], in_=grouped[g, u][:])
+            codes[g, u] = c
+            scales[g, u] = s
+
+        def multiply(g, u):
+            for q in range(SLOTS):
+                if g == 0:
+                    bank = (u * SLOTS + q) % BANKS
+                    acc[u, q] = psum.tile([P, N], F32, name="acc%d" % bank)
+                cols = slice(q * P, (q + 1) * P)
+                rhs = w8[:].bitcast(FP8X4) if g == 0 else w4[:, g - 1, :].bitcast(FP4X4)
+                nc.tensor.matmul_mx(
+                    out=acc[u, q][:],
+                    lhsT=codes[g, u][:, cols].bitcast(FP8X4),
+                    lhsT_scale=scales[g, u][:, cols],
+                    rhs=rhs,
+                    rhs_scale=w_scale[:, g, :],
+                    start=(g == 0),
+                    stop=(g == PASSES - 1),
+                )
+
+        def add(u):
+            for q in range(SLOTS):
+                nc.vector.tensor_add(out=o_sb[u][:, q, :], in0=acc[u, q][:], in1=r_sb[u][:, q, :])
+
+        def prepare(g, first, count):
+            copy(g, first)
+            for u in range(first + 1, first + count):
+                copy(g, u)
+                quantise(g, u - 1)
+            quantise(g, first + count - 1)
+
+        nc.gpsimd.memset(w_scale[:].rearrange("p g n -> p (g n)").bitcast(I32), 0)
+        load_x(0, 0, 3)
+        nc.sync.dma_start(out=w8[:].bitcast(I32), in_=w8_words[0].rearrange("p n i -> p (n i)").bitcast(I32))
+        nc.sync.dma_start(out=w4[:].bitcast(I32), in_=w4_words.rearrange("g p b -> p g b").bitcast(I32))
+        for quad in range(4):
+            rows = slice(32 * quad, 32 * quad + 4)
+            quad_rows = slice(4 * quad, 4 * quad + 4)
+            nc.gpsimd.dma_start(out=w_scale[rows, 0, :].bitcast(I32), in_=w8_scales[0, quad_rows, :].bitcast(I32))
+        for quad in range(4):
+            rows = slice(32 * quad, 32 * quad + 4)
+            quad_rows = slice(4 * quad, 4 * quad + 4)
+            nc.gpsimd.dma_start(
+                out=w_scale[rows, 1:, :].bitcast(I32),
+                in_=w4_scales[:, quad_rows, :].rearrange("g s n -> s g n").bitcast(I32),
+            )
+        load_x(1, 0, 3)
+        load_x(2, 0, 2)
+        load_x(3, 0, 2)
+        load_r(0, 0, 4)
+        load_r(1, 0, 4)
+        load_x(2, 2, 1)
+        load_x(3, 2, 1)
+        load_r(2, 0, 2)
+        load_r(2, 2, 2)
+
+        for g in (0, 1):
+            prepare(g, 0, 3)
+            multiply(g, 0)
+            multiply(g, 1)
+        for g in (2, 3):
+            prepare(g, 0, 2)
+            multiply(g, 0)
+            multiply(g, 1)
+        add(0)
+        store(0, 0, 4)
+        multiply(0, 2)
+        multiply(1, 2)
+        add(1)
+        store(1, 0, 4)
+        for g in (2, 3):
+            prepare(g, 2, 1)
+            multiply(g, 2)
+        add(2)
+        store(2, 0, 2)
+        store(2, 2, 1)
+        store(2, 3, 1)

@@ -20,6 +20,7 @@ SLOTS = UNIT // P
 UNITS = T // UNIT
 BANKS = 8
 VECTOR_M = 80
+ORDER = (1, 2, 3, 0)
 
 FLOPS = 2 * K * T * N
 
@@ -59,7 +60,8 @@ def tile_mix_outl_tm_res_kernel(tc, x, w8_words, w8_scales, w4_words, w4_scales,
             o_sb[u] = keep.tile([P, SLOTS, N], F32, name="o%d" % u)
         w8 = keep.tile([P, 4 * N], U8, name="w8", align_bytes=64)
         w4 = keep.tile([P, PASSES - 1, 2 * N], U8, name="w4", align_bytes=64)
-        w_scale = keep.tile([P, PASSES, N], U8, name="w_scale", align_bytes=64)
+        w8_scale = keep.tile([P, N], U8, name="w8_scale", align_bytes=64)
+        w4_scale = keep.tile([P, PASSES - 1, N], U8, name="w4_scale", align_bytes=64)
 
         def copy(g, u):
             t = keep.tile([P, UNIT * PACK], BF16, name="b%d_%d" % (g, u), align_bytes=64)
@@ -78,7 +80,7 @@ def tile_mix_outl_tm_res_kernel(tc, x, w8_words, w8_scales, w4_words, w4_scales,
 
         def multiply(g, u):
             for q in range(SLOTS):
-                if g == 0:
+                if g == ORDER[0]:
                     bank = (u * SLOTS + q) % BANKS
                     acc[u, q] = psum.tile([P, N], F32, name="acc%d" % bank)
                 cols = slice(q * P, (q + 1) * P)
@@ -88,9 +90,9 @@ def tile_mix_outl_tm_res_kernel(tc, x, w8_words, w8_scales, w4_words, w4_scales,
                     lhsT=codes[g, u][:, cols].bitcast(FP8X4),
                     lhsT_scale=scales[g, u][:, cols],
                     rhs=rhs,
-                    rhs_scale=w_scale[:, g, :],
-                    start=(g == 0),
-                    stop=(g == PASSES - 1),
+                    rhs_scale=w8_scale[:] if g == 0 else w4_scale[:, g - 1, :],
+                    start=(g == ORDER[0]),
+                    stop=(g == ORDER[-1]),
                 )
 
         def add(u):
@@ -104,46 +106,46 @@ def tile_mix_outl_tm_res_kernel(tc, x, w8_words, w8_scales, w4_words, w4_scales,
                 quantise(g, u - 1)
             quantise(g, first + count - 1)
 
-        nc.gpsimd.memset(w_scale[:].rearrange("p g n -> p (g n)").bitcast(I32), 0)
-        load_x(0, 0, 3)
-        nc.sync.dma_start(out=w8[:].bitcast(I32), in_=w8_words[0].rearrange("p n i -> p (n i)").bitcast(I32))
+        nc.vector.memset(w4_scale[:].rearrange("p g n -> p (g n)").bitcast(I32), 0)
+        nc.vector.memset(w8_scale[:].bitcast(I32), 0)
         nc.sync.dma_start(out=w4[:].bitcast(I32), in_=w4_words.rearrange("g p b -> p g b").bitcast(I32))
         for quad in range(4):
-            rows = slice(32 * quad, 32 * quad + 4)
-            quad_rows = slice(4 * quad, 4 * quad + 4)
-            nc.gpsimd.dma_start(out=w_scale[rows, 0, :].bitcast(I32), in_=w8_scales[0, quad_rows, :].bitcast(I32))
-        for quad in range(4):
-            rows = slice(32 * quad, 32 * quad + 4)
-            quad_rows = slice(4 * quad, 4 * quad + 4)
-            nc.gpsimd.dma_start(
-                out=w_scale[rows, 1:, :].bitcast(I32),
-                in_=w4_scales[:, quad_rows, :].rearrange("g s n -> s g n").bitcast(I32),
+            nc.sync.dma_start(
+                out=w4_scale[32 * quad : 32 * quad + 4, :, :].bitcast(I32),
+                in_=w4_scales[:, 4 * quad : 4 * quad + 4, :].rearrange("g s n -> s g n").bitcast(I32),
             )
-        load_x(1, 0, 3)
-        load_x(2, 0, 2)
-        load_x(3, 0, 2)
+        load_x(ORDER[0], 0, 3)
+        load_x(ORDER[1], 0, 3)
+        nc.sync.dma_start(out=w8[:].bitcast(I32), in_=w8_words[0].rearrange("p n i -> p (n i)").bitcast(I32))
+        for quad in range(4):
+            nc.sync.dma_start(
+                out=w8_scale[32 * quad : 32 * quad + 4, :].bitcast(I32),
+                in_=w8_scales[0, 4 * quad : 4 * quad + 4, :].bitcast(I32),
+            )
+        load_x(ORDER[2], 0, 2)
+        load_x(ORDER[3], 0, 2)
         load_r(0, 0, 4)
         load_r(1, 0, 4)
-        load_x(2, 2, 1)
-        load_x(3, 2, 1)
+        load_x(ORDER[2], 2, 1)
+        load_x(ORDER[3], 2, 1)
         load_r(2, 0, 2)
         load_r(2, 2, 2)
 
-        for g in (0, 1):
+        for g in ORDER[:2]:
             prepare(g, 0, 3)
             multiply(g, 0)
             multiply(g, 1)
-        for g in (2, 3):
+        for g in ORDER[2:]:
             prepare(g, 0, 2)
             multiply(g, 0)
             multiply(g, 1)
         add(0)
         store(0, 0, 4)
-        multiply(0, 2)
-        multiply(1, 2)
+        multiply(ORDER[0], 2)
+        multiply(ORDER[1], 2)
         add(1)
         store(1, 0, 4)
-        for g in (2, 3):
+        for g in ORDER[2:]:
             prepare(g, 2, 1)
             multiply(g, 2)
         add(2)

from contextlib import ExitStack

import concourse.mybir as mybir

F32 = mybir.dt.float32
BF16 = mybir.dt.bfloat16
I32 = mybir.dt.int32
U32 = mybir.dt.uint32
U8 = mybir.dt.uint8
FP8X4 = mybir.dt.float8_e4m3fn_x4
FP4X4 = mybir.dt.float4_e2m1fn_x4

P = 128
K, T, N = 2048, 1536, 512
PACK = 4
K_PASS = P * PACK
PASSES = K // K_PASS
UNIT = 512
SLOTS = UNIT // P
UNITS = T // UNIT
BANKS = 8
VECTOR_M = 80
ORDER = (1, 2, 3, 0)

FLOPS = 2 * K * T * N


def tile_mix_outl_tm_res_kernel(tc, x, w8_words, w8_scales, w4_words, w4_scales, r, out):
    nc = tc.nc
    with ExitStack() as ctx:
        keep = ctx.enter_context(tc.tile_pool(name="keep", bufs=1))
        psum = ctx.enter_context(tc.psum_pool(name="psum", bufs=1))
        ctx.enter_context(tc.manual_schedule())

        def load_x(g, first, count):
            width = count * UNIT
            t = keep.tile([P, PACK, width], F32, name="x%d_%d" % (g, first))
            rows = x[g * K_PASS : (g + 1) * K_PASS, :].rearrange("(p i) t -> p i t", i=PACK)
            nc.sync.dma_start(out=t[:], in_=rows[:, :, first * UNIT : first * UNIT + width])
            for u in range(first, first + count):
                raw[g, u] = t[:, :, (u - first) * UNIT : (u - first + 1) * UNIT]

        def load_r(u, first, count):
            rows = r[u * UNIT : (u + 1) * UNIT, :].rearrange("(m q) n -> m q n", q=SLOTS)
            nc.sync.dma_start(out=r_sb[u][:, first : first + count, :], in_=rows[:, first : first + count, :])

        def store(u, first, count):
            rows = out[u * UNIT : (u + 1) * UNIT, :].rearrange("(m q) n -> m q n", q=SLOTS)
            nc.sync.dma_start(out=rows[:, first : first + count, :], in_=o_sb[u][:, first : first + count, :])

        raw = {}
        grouped = {}
        codes = {}
        scales = {}
        r_sb = {}
        o_sb = {}
        acc = {}
        for u in range(UNITS):
            r_sb[u] = keep.tile([P, SLOTS, N], F32, name="r%d" % u)
            o_sb[u] = keep.tile([P, SLOTS, N], F32, name="o%d" % u)
        w8 = keep.tile([P, 4 * N], U8, name="w8", align_bytes=64)
        w4 = keep.tile([P, PASSES - 1, 2 * N], U8, name="w4", align_bytes=64)
        w8_scale = keep.tile([P, N], U8, name="w8_scale", align_bytes=64)
        w4_scale = keep.tile([P, PASSES - 1, N], U8, name="w4_scale", align_bytes=64)

        def copy(g, u):
            t = keep.tile([P, UNIT * PACK], BF16, name="b%d_%d" % (g, u), align_bytes=64)
            dst = t[:].rearrange("p (q m i) -> p m i q", q=SLOTS, i=PACK)
            src = raw[g, u].rearrange("p i (m q) -> p m i q", q=SLOTS)
            nc.vector.tensor_copy(out=dst[:, :VECTOR_M], in_=src[:, :VECTOR_M])
            nc.scalar.copy(out=dst[:, VECTOR_M:], in_=src[:, VECTOR_M:])
            grouped[g, u] = t

        def quantise(g, u):
            c = keep.tile([P, UNIT], U32, name="c%d_%d" % (g, u), align_bytes=64)
            s = keep.tile([P, UNIT], U8, name="s%d_%d" % (g, u), align_bytes=64)
            nc.vector.quantize_mx(out=c[:].bitcast(FP8X4), scales=s[:], in_=grouped[g, u][:])
            codes[g, u] = c
            scales[g, u] = s

        def multiply(g, u):
            for q in range(SLOTS):
                if g == ORDER[0]:
                    bank = (u * SLOTS + q) % BANKS
                    acc[u, q] = psum.tile([P, N], F32, name="acc%d" % bank)
                cols = slice(q * P, (q + 1) * P)
                rhs = w8[:].bitcast(FP8X4) if g == 0 else w4[:, g - 1, :].bitcast(FP4X4)
                nc.tensor.matmul_mx(
                    out=acc[u, q][:],
                    lhsT=codes[g, u][:, cols].bitcast(FP8X4),
                    lhsT_scale=scales[g, u][:, cols],
                    rhs=rhs,
                    rhs_scale=w8_scale[:] if g == 0 else w4_scale[:, g - 1, :],
                    start=(g == ORDER[0]),
                    stop=(g == ORDER[-1]),
                )

        def add(u):
            for q in range(SLOTS):
                nc.vector.tensor_add(out=o_sb[u][:, q, :], in0=acc[u, q][:], in1=r_sb[u][:, q, :])

        def prepare(g, first, count):
            copy(g, first)
            for u in range(first + 1, first + count):
                copy(g, u)
                quantise(g, u - 1)
            quantise(g, first + count - 1)

        nc.vector.memset(w4_scale[:].rearrange("p g n -> p (g n)").bitcast(I32), 0)
        nc.vector.memset(w8_scale[:].bitcast(I32), 0)
        nc.sync.dma_start(out=w4[:].bitcast(I32), in_=w4_words.rearrange("g p b -> p g b").bitcast(I32))
        for quad in range(4):
            nc.sync.dma_start(
                out=w4_scale[32 * quad : 32 * quad + 4, :, :].bitcast(I32),
                in_=w4_scales[:, 4 * quad : 4 * quad + 4, :].rearrange("g s n -> s g n").bitcast(I32),
            )
        load_x(ORDER[0], 0, 3)
        load_x(ORDER[1], 0, 3)
        nc.sync.dma_start(out=w8[:].bitcast(I32), in_=w8_words[0].rearrange("p n i -> p (n i)").bitcast(I32))
        for quad in range(4):
            nc.sync.dma_start(
                out=w8_scale[32 * quad : 32 * quad + 4, :].bitcast(I32),
                in_=w8_scales[0, 4 * quad : 4 * quad + 4, :].bitcast(I32),
            )
        load_x(ORDER[2], 0, 2)
        load_x(ORDER[3], 0, 2)
        load_r(0, 0, 4)
        load_r(1, 0, 4)
        load_x(ORDER[2], 2, 1)
        load_x(ORDER[3], 2, 1)
        load_r(2, 0, 2)
        load_r(2, 2, 2)

        for g in ORDER[:2]:
            prepare(g, 0, 3)
            multiply(g, 0)
            multiply(g, 1)
        for g in ORDER[2:]:
            prepare(g, 0, 2)
            multiply(g, 0)
            multiply(g, 1)
        add(0)
        store(0, 0, 4)
        multiply(ORDER[0], 2)
        multiply(ORDER[1], 2)
        add(1)
        store(1, 0, 4)
        for g in ORDER[2:]:
            prepare(g, 2, 1)
            multiply(g, 2)
        add(2)
        store(2, 0, 2)
        store(2, 2, 1)
        store(2, 3, 1)
